import numpy as np
import ml_dtypes


def mxq(x, axis, fmt="e4m3"):
    dtype, down = {"e4m3": (ml_dtypes.float8_e4m3fn, 7), "e5m2": (ml_dtypes.float8_e5m2, 14)}[fmt]
    v = np.moveaxis(np.asarray(x, np.float32).astype(ml_dtypes.bfloat16).astype(np.float64), axis, -1)
    blocks = v.reshape(v.shape[:-1] + (-1, 32))
    amax = np.abs(blocks).max(-1, keepdims=True)
    byte = np.maximum(np.where(amax > 0, np.frexp(amax)[1] - 1 + 127, 0) - down, 1)
    scale = np.exp2(byte - 127.0)
    codes = (blocks / scale).astype(np.float32).astype(dtype).astype(np.float64)
    return np.moveaxis((codes * scale).reshape(v.shape), -1, axis)


WIDE = False


def mx_kscale(k):
    if not WIDE:
        return np.ones(k)
    levels = np.array([10, -10, 5, -5, 0])
    if k % 512:
        return np.exp2(np.random.permutation(np.resize(levels, k // 32))).repeat(32)
    a = np.empty((k // 512, 16))
    for p in range(k // 512):
        a[p, :8] = np.random.permutation(np.resize(levels, 8))
        for g in range(8):
            far = levels[np.abs(levels - a[p, g]) >= 10]
            a[p, g + 8] = far[np.random.randint(len(far))]
    return np.exp2(a.ravel()).repeat(32)


def f64(x):
    return np.asarray(x).astype(np.float64)


def striped(idx):
    return np.tile(idx.reshape(-1, 16).T, (8, 1)).astype(np.uint16)


def unstriped(offs):
    return offs[:16].T.reshape(-1).astype(np.int64)


def relu(v):
    return np.maximum(v, 0.0)

def planes(y):
    n, m = y.shape
    v = y.astype(np.float32).astype(ml_dtypes.bfloat16).astype(np.float64).reshape(n // 32, 32, m)
    top = np.abs(v).max(1)
    byte = np.clip(np.where(top > 0, np.frexp(top)[1] - 1 + 127 - 7, 1), 1, 254)
    codes = (v * np.exp2(127.0 - byte)[:, None, :]).reshape(n, m).astype(np.float32).astype(ml_dtypes.float8_e4m3fn).view(np.uint8)
    words = codes.reshape(n // 512, 128, 4, m).transpose(0, 1, 3, 2)
    return np.ascontiguousarray(words), np.ascontiguousarray(byte.astype(np.uint8).reshape(n // 512, 16, m))


K, T, S, D, V, H, U = 512, 2048, 1024, 2, 512, 512, 256
P = 2 ** 7


def setup_inputs():
    n = np.random.standard_normal
    s = mx_kscale(K)[:, None]
    u = mx_kscale(H)
    return {
        "xT": (n((K, T)) * s).astype(np.float32),
        "w1": (n((K, H)) / np.sqrt(K) / s * u).astype(np.float32),
        "w2": (n((H, H)) / np.sqrt(H) / u[:, None]).astype(np.float32),
        "gate": (np.tile(np.random.uniform(0.2, 1.0, (D, 1, V)) / np.sqrt(D), (1, P, 1))).astype(np.float32),
        "gate2": (np.tile(np.random.uniform(0.2, 1.0, (D, 1, U)) / np.sqrt(D), (1, P, 1))).astype(np.float32),
        "offs": striped(np.random.permutation(T)[:S]),
        "pos1": striped(np.random.permutation(S)[:V]),
        "pos2": striped(np.random.permutation(S)[:V]),
        "nxt1": striped(np.random.permutation(V)[:U]),
        "nxt2": striped(np.random.permutation(V)[:U]),
    }


def reference(xT, w1, w2, gate, gate2, offs, pos1, pos2, nxt1, nxt2):
    xq = mxq(f64(xT)[:, unstriped(offs)], 0, "e4m3")
    h = relu(mxq(f64(w1), 0, "e4m3").T @ xq)
    z = h[:, unstriped(pos1)] * f64(gate)[0, :1] + h[:, unstriped(pos2)] * f64(gate)[1, :1]
    g = relu(mxq(f64(w2), 0, "e4m3").T @ mxq(z, 0, "e4m3"))
    out_0 = g[:, unstriped(nxt1)] * f64(gate2)[0, :1] + g[:, unstriped(nxt2)] * f64(gate2)[1, :1]
    return (out_0,) + planes(out_0)

@@ -1,0 +1,163 @@
+from contextlib import ExitStack
+
+import concourse.mybir as mybir
+
+K, T, S, V, H, U = 512, 2048, 1024, 512, 512, 256
+FLOPS = 2 * K * H * S + 2 * H * H * V
+
+F32 = mybir.dt.float32
+BF16 = mybir.dt.bfloat16
+I32 = mybir.dt.int32
+U32 = mybir.dt.uint32
+U16 = mybir.dt.uint16
+U8 = mybir.dt.uint8
+FP8X4 = mybir.dt.float8_e4m3fn_x4
+ACT = mybir.ActivationFunctionType
+ALU = mybir.AluOpType
+
+P = 128
+PACK = 4
+HALF_S = S // 2
+HALF_V = V // 2
+HALF_H = H // 2
+
+HOP1_ON_SCALAR = [(0, 2, 0), (0, 3, 0), (1, 0, 0), (1, 0, 1), (1, 1, 0), (1, 1, 1), (1, 2, 0), (1, 2, 1), (1, 3, 0)]
+HOP2_ON_SCALAR = [(0, 0), (1, 0), (1, 1), (2, 0), (2, 1), (3, 0)]
+
+
+def tile_picked_hop2_relu_lo_kernel(tc, xT, w1, w2, gate, gate2, offs, pos1, pos2, nxt1, nxt2, out_0, out_1, out_2):
+    nc = tc.nc
+    with ExitStack() as ctx:
+        sb = ctx.enter_context(tc.tile_pool(name="sb", bufs=1))
+        ps = ctx.enter_context(tc.psum_pool(name="ps", bufs=1))
+
+        def load(name, shape, dtype, src):
+            dst = sb.tile(shape, dtype, name=name)
+            nc.sync.dma_start(dst[:], src)
+            return dst
+
+        def mx_tiles(name, width):
+            codes = sb.tile([P, width], U32, name=name + "_codes", align_bytes=64)
+            scales = sb.tile([P, width], U8, name=name + "_scales", align_bytes=64)
+            return codes, scales
+
+        def quantise(codes, scales, src):
+            nc.vector.quantize_mx(out=codes.bitcast(FP8X4), scales=scales, in_=src)
+
+        def weave(copy, dst, src):
+            copy(dst.rearrange("p (c i t) -> p c t i", i=2, t=PACK), src.rearrange("p t (c i) -> p c t i", i=2))
+
+        def deal(dst, raw, first, count):
+            nc.vector.tensor_copy(
+                dst[:].rearrange("p (t m a b) -> p m a t b", t=PACK, a=2, b=2)[:, first:first + count],
+                raw[:].rearrange("p (a b) (m t) -> p m a t b", a=2, t=PACK),
+            )
+
+        x_rows = xT.rearrange("(p j) n -> p j n", j=PACK)
+        w1_rows = w1.rearrange("(p j) c -> p j c", j=PACK)
+        offs_sb = load("offs_sb", [P, S // 16], U16, offs)
+        x_sb = [load("x_sb%d" % j, [P, T], F32, x_rows[:, j, :]) for j in range(PACK)]
+        w1_raw = [load("w1_raw%d" % a, [P, PACK, HALF_H], F32, w1_rows[:, :, a * HALF_H:(a + 1) * HALF_H]) for a in range(2)]
+        w2_raw = load("w2_raw", [P, PACK, H], F32, w2.rearrange("(p j) c -> p j c", j=PACK))
+        pos_sb = [load("pos1_sb", [P, V // 16], U16, pos1), load("pos2_sb", [P, V // 16], U16, pos2)]
+        gate_rows = gate.rearrange("d p v -> p d v")
+        gate_sb = [load("gate_sb%d" % a, [P, 2, HALF_V], F32, gate_rows[:, :, a * HALF_V:(a + 1) * HALF_V]) for a in range(2)]
+        nxt_sb = [load("nxt1_sb", [P, U // 16], U16, nxt1), load("nxt2_sb", [P, U // 16], U16, nxt2)]
+        gate2_sb = load("gate2_sb", [P, 2, U], F32, gate2.rearrange("d p r -> p d r"))
+
+        x_bf = [sb.tile([P, HALF_S * PACK], BF16, name="x_bf%d" % a, align_bytes=64) for a in range(2)]
+        x_picked = sb.tile([P, PACK, HALF_S], F32, name="x_picked")
+        cols = HALF_S // 16
+        for j in range(PACK):
+            nc.vector.tensor_copy(x_bf[0][:].rearrange("p (n j) -> p n j", j=PACK)[:, :, j], x_sb[j][:].indirect(offs_sb[:, 0:cols]))
+            nc.scalar.activation(x_picked[:, j, :], x_sb[j][:].indirect(offs_sb[:, cols:2 * cols]), ACT.Copy)
+        x_mx = [mx_tiles("x%d" % a, HALF_S) for a in range(2)]
+        quantise(x_mx[0][0][:], x_mx[0][1][:], x_bf[0][:])
+        weave(nc.scalar.copy, x_bf[1][:], x_picked[:])
+
+        w1_bf = sb.tile([P, H * PACK], BF16, name="w1_bf", align_bytes=64)
+        for a in range(2):
+            deal(w1_bf, w1_raw[a], a * (P // 2), P // 2)
+        w1_codes, w1_scales = mx_tiles("w1", H)
+        for t in range(PACK):
+            quantise(w1_codes[:, t * P:(t + 1) * P], w1_scales[:, t * P:(t + 1) * P], w1_bf[:, t * H:(t + 1) * H])
+        quantise(x_mx[1][0][:], x_mx[1][1][:], x_bf[1][:])
+
+        w2_bf = sb.tile([P, H * PACK], BF16, name="w2_bf", align_bytes=64)
+        deal(w2_bf, w2_raw, 0, P)
+
+        def product(bank, width, w_codes, w_scales, t, moving):
+            acc = ps.tile([P, width], F32, name="acc", tag="bank%d" % bank)
+            nc.tensor.matmul_mx(
+                out=acc[:], lhsT=w_codes[:, t * P:(t + 1) * P].bitcast(FP8X4), lhsT_scale=w_scales[:, t * P:(t + 1) * P],
+                rhs=moving[0][:].bitcast(FP8X4), rhs_scale=moving[1][:], start=True, stop=True)
+            return acc
+
+        h_sb = [sb.tile([P, S], F32, name="h_sb%d" % t) for t in range(PACK)]
+        for t, a in [(0, 0), (1, 0), (0, 1), (1, 1), (2, 0), (2, 1), (3, 0), (3, 1)]:
+            acc = product(2 * t + a, HALF_S, w1_codes, w1_scales, t, x_mx[a])
+            nc.scalar.activation(h_sb[t][:, a * HALF_S:(a + 1) * HALF_S], acc[:], ACT.Relu)
+
+        def fetch(on_scalar, term, plain, window, offsets):
+            if on_scalar:
+                nc.scalar.activation(plain, window[:].indirect(offsets), ACT.Copy)
+
+        def weigh(on_scalar, term, plain, window, offsets, weight):
+            src = plain if on_scalar else window[:].indirect(offsets)
+            nc.vector.tensor_tensor(term, src, weight, ALU.mult)
+
+        w2_codes, w2_scales = mx_tiles("w2", H)
+        g_sb = [sb.tile([P, V], F32, name="g_sb%d" % t) for t in range(PACK)]
+        cols = HALF_V // 16
+        g_acc = {}
+        for a in range(2):
+            terms = [sb.tile([P, PACK, HALF_V], F32, name="z_term%d%d" % (a, d)) for d in range(2)]
+            plain = [sb.tile([P, PACK, HALF_V], F32, name="z_plain%d%d" % (a, d)) for d in range(2)]
+            jobs = [(t, d) for t in range(PACK) for d in range(2)]
+            for t, d in jobs:
+                fetch((a, t, d) in HOP1_ON_SCALAR, terms[d][:, t, :], plain[d][:, t, :], h_sb[t], pos_sb[d][:, a * cols:(a + 1) * cols])
+            jobs = sorted(jobs, key=lambda job: (a, job[0], job[1]) in HOP1_ON_SCALAR)
+            for t, d in jobs:
+                weigh((a, t, d) in HOP1_ON_SCALAR, terms[d][:, t, :], plain[d][:, t, :], h_sb[t], pos_sb[d][:, a * cols:(a + 1) * cols], gate_sb[a][:, d, :])
+            if a == 0:
+                quantise(w2_codes[:], w2_scales[:], w2_bf[:])
+            z_bf = sb.tile([P, HALF_V * PACK], BF16, name="z_bf%d" % a, align_bytes=64)
+            nc.vector.tensor_tensor(
+                z_bf[:].rearrange("p (c i t) -> p c t i", i=2, t=PACK),
+                terms[0][:].rearrange("p t (c i) -> p c t i", i=2),
+                terms[1][:].rearrange("p t (c i) -> p c t i", i=2), ALU.add)
+            z_mx = mx_tiles("z%d" % a, HALF_V)
+            quantise(z_mx[0][:], z_mx[1][:], z_bf[:])
+            for t in range(PACK):
+                g_acc[a, t] = product(2 * t + a, HALF_V, w2_codes, w2_scales, t, z_mx)
+        for a in range(2):
+            for t in range(PACK):
+                dst = g_sb[t][:, a * HALF_V:(a + 1) * HALF_V]
+                if a == 1 and t == 0:
+                    nc.vector.tensor_scalar_max(dst, g_acc[a, t][:], 0.0)
+                else:
+                    nc.scalar.activation(dst, g_acc[a, t][:], ACT.Relu)
+
+        terms = [sb.tile([P, PACK, U], F32, name="y_term%d" % d) for d in range(2)]
+        plain = [sb.tile([P, PACK, U], F32, name="y_plain%d" % d) for d in range(2)]
+        y_sb = sb.tile([P, PACK, U], F32, name="y_sb")
+        y_rows = out_0.rearrange("(p t) r -> p t r", t=PACK)
+        for t in range(PACK):
+            for d in range(2):
+                fetch((t, d) in HOP2_ON_SCALAR, terms[d][:, t, :], plain[d][:, t, :], g_sb[t], nxt_sb[d][:])
+        for t, d in [(0, 1), (3, 1), (0, 0), (1, 0), (1, 1), (2, 0), (2, 1), (3, 0)]:
+            weigh((t, d) in HOP2_ON_SCALAR, terms[d][:, t, :], plain[d][:, t, :], g_sb[t], nxt_sb[d][:], gate2_sb[:, d, :])
+            if (t, d) in [(1, 1), (3, 0)]:
+                pair = slice(t - 1, t + 1)
+                nc.vector.tensor_tensor(y_sb[:, pair, :], terms[0][:, pair, :], terms[1][:, pair, :], ALU.add)
+                nc.sync.dma_start(y_rows[:, pair, :], y_sb[:, pair, :])
+
+        y_bf = sb.tile([P, U * PACK], BF16, name="y_bf", align_bytes=64)
+        weave(nc.vector.tensor_copy, y_bf[:], y_sb[:])
+        y_codes, y_scales = mx_tiles("y", U)
+        quantise(y_codes[:], y_scales[:], y_bf[:])
+        nc.sync.dma_start(out_1[0].rearrange("l c r -> l (c r)").bitcast(I32), y_codes[:].bitcast(I32))
+        scale_rows = out_2[0].bitcast(I32)
+        for q in range(4):
+            queue = nc.sync if q % 2 else nc.scalar
+            queue.dma_start(scale_rows[4 * q:4 * q + 4, :], y_scales[:].bitcast(I32)[32 * q:32 * q + 4, :])

@@ -18,11 +18,11 @@ ALU = mybir.AluOpType
 P = 128
 PACK = 4
 HALF_S = S // 2
-HALF_V = V // 2
 HALF_H = H // 2
-
-HOP1_ON_SCALAR = [(0, 2, 0), (0, 3, 0), (1, 0, 0), (1, 0, 1), (1, 1, 0), (1, 1, 1), (1, 2, 0), (1, 2, 1), (1, 3, 0)]
-HOP2_ON_SCALAR = [(0, 0), (1, 0), (1, 1), (2, 0), (2, 1), (3, 0)]
+HOP1_PARTS = [(0, 256, [(0,0),(0,1),(1,0),(1,1),(2,0),(2,1),(3,1)]), (256, 128, []), (384,128,[])]
+HOP2_PARTS = [(0,128,[(0,0),(0,1),(1,0),(1,1)]),(128,128,[(0,0),(0,1)])]
+H_BANKS_ON_VECTOR = []
+G_BANKS_ON_VECTOR = [0]
 
 
 def tile_picked_hop2_relu_lo_kernel(tc, xT, w1, w2, gate, gate2, offs, pos1, pos2, nxt1, nxt2, out_0, out_1, out_2):
@@ -32,131 +32,139 @@ def tile_picked_hop2_relu_lo_kernel(tc, xT, w1, w2, gate, gate2, offs, pos1, pos
         ps = ctx.enter_context(tc.psum_pool(name="ps", bufs=1))
 
         def load(name, shape, dtype, src):
-            dst = sb.tile(shape, dtype, name=name)
+            dst = sb.tile(shape, dtype, name=name, tag=name, align_bytes=64)
             nc.sync.dma_start(dst[:], src)
             return dst
 
-        def mx_tiles(name, width):
-            codes = sb.tile([P, width], U32, name=name + "_codes", align_bytes=64)
+        def mx_tiles(name, width, after=None):
+            codes = sb.tile([P, width], U32, name=name + "_codes", tag=after or name + "_codes", align_bytes=64)
             scales = sb.tile([P, width], U8, name=name + "_scales", align_bytes=64)
             return codes, scales
 
         def quantise(codes, scales, src):
-            nc.vector.quantize_mx(out=codes.bitcast(FP8X4), scales=scales, in_=src)
+            n = codes.shape[1]
+            for c0, c1 in ([(0, 128), (128, 192)] if n == 192 else [(0, n)]):
+                nc.vector.quantize_mx(out=codes[:, c0:c1].bitcast(FP8X4), scales=scales[:, c0:c1], in_=src[:, 4 * c0:4 * c1])
 
-        def weave(copy, dst, src):
-            copy(dst.rearrange("p (c i t) -> p c t i", i=2, t=PACK), src.rearrange("p t (c i) -> p c t i", i=2))
-
-        def deal(dst, raw, first, count):
-            nc.vector.tensor_copy(
-                dst[:].rearrange("p (t m a b) -> p m a t b", t=PACK, a=2, b=2)[:, first:first + count],
-                raw[:].rearrange("p (a b) (m t) -> p m a t b", a=2, t=PACK),
+        def deal(copy, dst, raw, first, count, ts=slice(0, PACK)):
+            copy(
+                dst[:].rearrange("p (t m a b) -> p m a t b", t=PACK, a=2, b=2)[:, first:first + count, :, ts, :],
+                raw[:].rearrange("p (a b) (m t) -> p m a t b", a=2, t=PACK)[:, :, :, ts, :],
             )
+
+        def relu(on_vector, dst, acc):
+            if on_vector:
+                nc.vector.tensor_scalar_max(dst, acc, 0.0)
+            else:
+                nc.scalar.activation(dst, acc, ACT.Relu)
 
         x_rows = xT.rearrange("(p j) n -> p j n", j=PACK)
         w1_rows = w1.rearrange("(p j) c -> p j c", j=PACK)
+        x_sb = [load("x_sb0", [P, T], F32, x_rows[:, 0, :])]
         offs_sb = load("offs_sb", [P, S // 16], U16, offs)
-        x_sb = [load("x_sb%d" % j, [P, T], F32, x_rows[:, j, :]) for j in range(PACK)]
+        x_sb.extend([load("x_sb%d" % j, [P, T], F32, x_rows[:, j, :]) for j in range(1, PACK)])
         w1_raw = [load("w1_raw%d" % a, [P, PACK, HALF_H], F32, w1_rows[:, :, a * HALF_H:(a + 1) * HALF_H]) for a in range(2)]
-        w2_raw = load("w2_raw", [P, PACK, H], F32, w2.rearrange("(p j) c -> p j c", j=PACK))
+        w2_rows = w2.rearrange("(p j) c -> p j c", j=PACK)
+        w2_raw = [load("w2_raw%d" % a, [P, PACK, HALF_H], F32, w2_rows[:, :, a * HALF_H:(a + 1) * HALF_H]) for a in range(2)]
         pos_sb = [load("pos1_sb", [P, V // 16], U16, pos1), load("pos2_sb", [P, V // 16], U16, pos2)]
         gate_rows = gate.rearrange("d p v -> p d v")
-        gate_sb = [load("gate_sb%d" % a, [P, 2, HALF_V], F32, gate_rows[:, :, a * HALF_V:(a + 1) * HALF_V]) for a in range(2)]
+        gate_sb = [load("gate_sb%d" % v0, [P, 2, n], F32, gate_rows[:, :, v0:v0 + n]) for v0, n, own in HOP1_PARTS]
         nxt_sb = [load("nxt1_sb", [P, U // 16], U16, nxt1), load("nxt2_sb", [P, U // 16], U16, nxt2)]
-        gate2_sb = load("gate2_sb", [P, 2, U], F32, gate2.rearrange("d p r -> p d r"))
+        gate2_rows = gate2.rearrange("d p r -> p d r")
+        gate2_sb = [load("gate2_sb%d" % r0, [P, 2, n], F32, gate2_rows[:, :, r0:r0 + n]) for r0, n, own in HOP2_PARTS]
 
         x_bf = [sb.tile([P, HALF_S * PACK], BF16, name="x_bf%d" % a, align_bytes=64) for a in range(2)]
-        x_picked = sb.tile([P, PACK, HALF_S], F32, name="x_picked")
         cols = HALF_S // 16
-        for j in range(PACK):
-            nc.vector.tensor_copy(x_bf[0][:].rearrange("p (n j) -> p n j", j=PACK)[:, :, j], x_sb[j][:].indirect(offs_sb[:, 0:cols]))
-            nc.scalar.activation(x_picked[:, j, :], x_sb[j][:].indirect(offs_sb[:, cols:2 * cols]), ACT.Copy)
-        x_mx = [mx_tiles("x%d" % a, HALF_S) for a in range(2)]
-        quantise(x_mx[0][0][:], x_mx[0][1][:], x_bf[0][:])
-        weave(nc.scalar.copy, x_bf[1][:], x_picked[:])
+        for pair in range(2):
+            picked = sb.tile([P, 2, HALF_S], BF16, name="x_picked%d" % pair)
+            for e in range(2):
+                j = 2 * pair + e
+                nc.vector.tensor_copy(x_bf[0][:].rearrange("p (n j) -> p n j", j=PACK)[:, :, j], x_sb[j][:].indirect(offs_sb[:, 0:cols]))
+                nc.scalar.activation(picked[:, e, :], x_sb[j][:].indirect(offs_sb[:, cols:2 * cols]), ACT.Copy)
+            nc.vector.tensor_copy(
+                x_bf[1][:].rearrange("p (n j) -> p n j", j=PACK)[:, :, 2 * pair:2 * pair + 2],
+                picked[:].rearrange("p e n -> p n e"))
+        x_mx = [mx_tiles("x0", HALF_S, "x_sb3"), mx_tiles("x1", HALF_S)]
+        for a in range(2):
+            quantise(x_mx[a][0][:], x_mx[a][1][:], x_bf[a][:])
 
         w1_bf = sb.tile([P, H * PACK], BF16, name="w1_bf", align_bytes=64)
-        for a in range(2):
-            deal(w1_bf, w1_raw[a], a * (P // 2), P // 2)
+        deal(nc.scalar.copy, w1_bf, w1_raw[0], 0, P // 2)
+        for t in range(0, PACK, 2):
+            deal(nc.scalar.copy, w1_bf, w1_raw[1], P // 2, P // 2, slice(t, t + 2))
         w1_codes, w1_scales = mx_tiles("w1", H)
         for t in range(PACK):
             quantise(w1_codes[:, t * P:(t + 1) * P], w1_scales[:, t * P:(t + 1) * P], w1_bf[:, t * H:(t + 1) * H])
-        quantise(x_mx[1][0][:], x_mx[1][1][:], x_bf[1][:])
 
         w2_bf = sb.tile([P, H * PACK], BF16, name="w2_bf", align_bytes=64)
-        deal(w2_bf, w2_raw, 0, P)
+        deal(nc.vector.tensor_copy, w2_bf, w2_raw[0], 0, P // 2)
+        deal(nc.vector.tensor_copy, w2_bf, w2_raw[1], P // 2, P // 2)
+        w2_codes, w2_scales = mx_tiles("w2", H)
+        quantise(w2_codes[:], w2_scales[:], w2_bf[:])
 
         def product(bank, width, w_codes, w_scales, t, moving):
             acc = ps.tile([P, width], F32, name="acc", tag="bank%d" % bank)
-            nc.tensor.matmul_mx(
-                out=acc[:], lhsT=w_codes[:, t * P:(t + 1) * P].bitcast(FP8X4), lhsT_scale=w_scales[:, t * P:(t + 1) * P],
-                rhs=moving[0][:].bitcast(FP8X4), rhs_scale=moving[1][:], start=True, stop=True)
+            for c0, c1 in {384: [(0, 256), (256, 384)], 192: [(0, 128), (128, 192)]}.get(width, [(0, width)]):
+                nc.tensor.matmul_mx(
+                    out=acc[:, c0:c1], lhsT=w_codes[:, t * P:(t + 1) * P].bitcast(FP8X4), lhsT_scale=w_scales[:, t * P:(t + 1) * P],
+                    rhs=moving[0][:, c0:c1].bitcast(FP8X4), rhs_scale=moving[1][:, c0:c1], start=True, stop=True)
             return acc
 
         h_sb = [sb.tile([P, S], F32, name="h_sb%d" % t) for t in range(PACK)]
-        for t, a in [(0, 0), (1, 0), (0, 1), (1, 1), (2, 0), (2, 1), (3, 0), (3, 1)]:
-            acc = product(2 * t + a, HALF_S, w1_codes, w1_scales, t, x_mx[a])
-            nc.scalar.activation(h_sb[t][:, a * HALF_S:(a + 1) * HALF_S], acc[:], ACT.Relu)
+        for t in range(PACK):
+            for a in range(2):
+                acc = product(2 * t + a, HALF_S, w1_codes, w1_scales, t, x_mx[a])
+                relu(2 * t + a in H_BANKS_ON_VECTOR, h_sb[t][:, a * HALF_S:(a + 1) * HALF_S], acc[:])
 
-        def fetch(on_scalar, term, plain, window, offsets):
-            if on_scalar:
-                nc.scalar.activation(plain, window[:].indirect(offsets), ACT.Copy)
-
-        def weigh(on_scalar, term, plain, window, offsets, weight):
-            src = plain if on_scalar else window[:].indirect(offsets)
-            nc.vector.tensor_tensor(term, src, weight, ALU.mult)
-
-        w2_codes, w2_scales = mx_tiles("w2", H)
-        g_sb = [sb.tile([P, V], F32, name="g_sb%d" % t) for t in range(PACK)]
-        cols = HALF_V // 16
-        g_acc = {}
-        for a in range(2):
-            terms = [sb.tile([P, PACK, HALF_V], F32, name="z_term%d%d" % (a, d)) for d in range(2)]
-            plain = [sb.tile([P, PACK, HALF_V], F32, name="z_plain%d%d" % (a, d)) for d in range(2)]
+        def weighted_terms(name, windows, lists, first, count, own, weights):
+            terms = sb.tile([P, PACK, 2, count], F32, name=name + "_terms")
+            plain = sb.tile([P, PACK, 2, count], F32, name=name + "_plain")
+            cols = slice(first // 16, (first + count) // 16)
             jobs = [(t, d) for t in range(PACK) for d in range(2)]
             for t, d in jobs:
-                fetch((a, t, d) in HOP1_ON_SCALAR, terms[d][:, t, :], plain[d][:, t, :], h_sb[t], pos_sb[d][:, a * cols:(a + 1) * cols])
-            jobs = sorted(jobs, key=lambda job: (a, job[0], job[1]) in HOP1_ON_SCALAR)
-            for t, d in jobs:
-                weigh((a, t, d) in HOP1_ON_SCALAR, terms[d][:, t, :], plain[d][:, t, :], h_sb[t], pos_sb[d][:, a * cols:(a + 1) * cols], gate_sb[a][:, d, :])
-            if a == 0:
-                quantise(w2_codes[:], w2_scales[:], w2_bf[:])
-            z_bf = sb.tile([P, HALF_V * PACK], BF16, name="z_bf%d" % a, align_bytes=64)
+                if (t, d) in own:
+                    nc.vector.tensor_tensor(terms[:, t, d, :], windows[t][:].indirect(lists[d][:, cols]), weights[:, d, :], ALU.mult)
+                else:
+                    nc.scalar.activation(plain[:, t, d, :], windows[t][:].indirect(lists[d][:, cols]), ACT.Copy)
+            for t in range(PACK):
+                rest = [d for d in range(2) if (t, d) not in own]
+                if rest:
+                    ds = slice(rest[0], rest[-1] + 1)
+                    nc.vector.tensor_tensor(terms[:, t, ds, :], plain[:, t, ds, :], weights[:, ds, :], ALU.mult)
+            return terms[:, :, 0, :], terms[:, :, 1, :]
+
+        g_sb = [sb.tile([P, V], F32, name="g_sb%d" % t) for t in range(PACK)]
+        g_acc = []
+        for a, (v0, n, own) in enumerate(HOP1_PARTS):
+            terms = weighted_terms("z%d" % a, h_sb, pos_sb, v0, n, own, gate_sb[a])
+            z_bf = sb.tile([P, n * PACK], BF16, name="z_bf%d" % a, align_bytes=64)
             nc.vector.tensor_tensor(
                 z_bf[:].rearrange("p (c i t) -> p c t i", i=2, t=PACK),
-                terms[0][:].rearrange("p t (c i) -> p c t i", i=2),
-                terms[1][:].rearrange("p t (c i) -> p c t i", i=2), ALU.add)
-            z_mx = mx_tiles("z%d" % a, HALF_V)
+                terms[0].rearrange("p t (c i) -> p c t i", i=2),
+                terms[1].rearrange("p t (c i) -> p c t i", i=2), ALU.add)
+            z_mx = mx_tiles("z%d" % a, n)
             quantise(z_mx[0][:], z_mx[1][:], z_bf[:])
-            for t in range(PACK):
-                g_acc[a, t] = product(2 * t + a, HALF_V, w2_codes, w2_scales, t, z_mx)
-        for a in range(2):
-            for t in range(PACK):
-                dst = g_sb[t][:, a * HALF_V:(a + 1) * HALF_V]
-                if a == 1 and t == 0:
-                    nc.vector.tensor_scalar_max(dst, g_acc[a, t][:], 0.0)
-                else:
-                    nc.scalar.activation(dst, g_acc[a, t][:], ACT.Relu)
+            g_acc.append([product((PACK * a + t) % 8, n, w2_codes, w2_scales, t, z_mx) for t in range(PACK)])
+            pass
+        for a, (v0, n, own) in enumerate(HOP1_PARTS):
+            last = a == len(HOP1_PARTS) - 1
+            if last or True:
+                for t in range(PACK):
+                    relu(last and t in G_BANKS_ON_VECTOR, g_sb[t][:, v0:v0 + n], g_acc[a][t][:])
 
-        terms = [sb.tile([P, PACK, U], F32, name="y_term%d" % d) for d in range(2)]
-        plain = [sb.tile([P, PACK, U], F32, name="y_plain%d" % d) for d in range(2)]
-        y_sb = sb.tile([P, PACK, U], F32, name="y_sb")
         y_rows = out_0.rearrange("(p t) r -> p t r", t=PACK)
-        for t in range(PACK):
-            for d in range(2):
-                fetch((t, d) in HOP2_ON_SCALAR, terms[d][:, t, :], plain[d][:, t, :], g_sb[t], nxt_sb[d][:])
-        for t, d in [(0, 1), (3, 1), (0, 0), (1, 0), (1, 1), (2, 0), (2, 1), (3, 0)]:
-            weigh((t, d) in HOP2_ON_SCALAR, terms[d][:, t, :], plain[d][:, t, :], g_sb[t], nxt_sb[d][:], gate2_sb[:, d, :])
-            if (t, d) in [(1, 1), (3, 0)]:
-                pair = slice(t - 1, t + 1)
-                nc.vector.tensor_tensor(y_sb[:, pair, :], terms[0][:, pair, :], terms[1][:, pair, :], ALU.add)
-                nc.sync.dma_start(y_rows[:, pair, :], y_sb[:, pair, :])
-
-        y_bf = sb.tile([P, U * PACK], BF16, name="y_bf", align_bytes=64)
-        weave(nc.vector.tensor_copy, y_bf[:], y_sb[:])
         y_codes, y_scales = mx_tiles("y", U)
-        quantise(y_codes[:], y_scales[:], y_bf[:])
-        nc.sync.dma_start(out_1[0].rearrange("l c r -> l (c r)").bitcast(I32), y_codes[:].bitcast(I32))
+        word_rows = out_1[0].rearrange("l c r -> l (c r)").bitcast(I32)
+        for a, (r0, n, own) in enumerate(HOP2_PARTS):
+            terms = weighted_terms("y%d" % a, g_sb, nxt_sb, r0, n, own, gate2_sb[a])
+            y_sb = sb.tile([P, PACK, n], F32, name="y_sb%d" % a)
+            nc.vector.tensor_tensor(y_sb[:], terms[0], terms[1], ALU.add)
+            nc.sync.dma_start(y_rows[:, :, r0:r0 + n], y_sb[:])
+            y_bf = sb.tile([P, n * PACK], BF16, name="y_bf%d" % a, align_bytes=64)
+            copy = nc.vector.tensor_copy if a == len(HOP2_PARTS) - 1 else nc.scalar.copy
+            copy(y_bf[:].rearrange("p (c i t) -> p c t i", i=2, t=PACK), y_sb[:].rearrange("p t (c i) -> p c t i", i=2))
+            quantise(y_codes[:, r0:r0 + n], y_scales[:, r0:r0 + n], y_bf[:])
+        nc.sync.dma_start(word_rows, y_codes[:].bitcast(I32))
         scale_rows = out_2[0].bitcast(I32)
         for q in range(4):
             queue = nc.sync if q % 2 else nc.scalar

from contextlib import ExitStack

import concourse.mybir as mybir

K, T, S, V, H, U = 512, 2048, 1024, 512, 512, 256
FLOPS = 2 * K * H * S + 2 * H * H * V

F32 = mybir.dt.float32
BF16 = mybir.dt.bfloat16
I32 = mybir.dt.int32
U32 = mybir.dt.uint32
U16 = mybir.dt.uint16
U8 = mybir.dt.uint8
FP8X4 = mybir.dt.float8_e4m3fn_x4
ACT = mybir.ActivationFunctionType
ALU = mybir.AluOpType

P = 128
PACK = 4
HALF_S = S // 2
HALF_H = H // 2
HOP1_PARTS = [(0, 256, [(0,0),(0,1),(1,0),(1,1),(2,0),(2,1),(3,1)]), (256, 128, []), (384,128,[])]
HOP2_PARTS = [(0,128,[(0,0),(0,1),(1,0),(1,1)]),(128,128,[(0,0),(0,1)])]
H_BANKS_ON_VECTOR = []
G_BANKS_ON_VECTOR = [0]


def tile_picked_hop2_relu_lo_kernel(tc, xT, w1, w2, gate, gate2, offs, pos1, pos2, nxt1, nxt2, out_0, out_1, out_2):
    nc = tc.nc
    with ExitStack() as ctx:
        sb = ctx.enter_context(tc.tile_pool(name="sb", bufs=1))
        ps = ctx.enter_context(tc.psum_pool(name="ps", bufs=1))

        def load(name, shape, dtype, src):
            dst = sb.tile(shape, dtype, name=name, tag=name, align_bytes=64)
            nc.sync.dma_start(dst[:], src)
            return dst

        def mx_tiles(name, width, after=None):
            codes = sb.tile([P, width], U32, name=name + "_codes", tag=after or name + "_codes", align_bytes=64)
            scales = sb.tile([P, width], U8, name=name + "_scales", align_bytes=64)
            return codes, scales

        def quantise(codes, scales, src):
            n = codes.shape[1]
            for c0, c1 in ([(0, 128), (128, 192)] if n == 192 else [(0, n)]):
                nc.vector.quantize_mx(out=codes[:, c0:c1].bitcast(FP8X4), scales=scales[:, c0:c1], in_=src[:, 4 * c0:4 * c1])

        def deal(copy, dst, raw, first, count, ts=slice(0, PACK)):
            copy(
                dst[:].rearrange("p (t m a b) -> p m a t b", t=PACK, a=2, b=2)[:, first:first + count, :, ts, :],
                raw[:].rearrange("p (a b) (m t) -> p m a t b", a=2, t=PACK)[:, :, :, ts, :],
            )

        def relu(on_vector, dst, acc):
            if on_vector:
                nc.vector.tensor_scalar_max(dst, acc, 0.0)
            else:
                nc.scalar.activation(dst, acc, ACT.Relu)

        x_rows = xT.rearrange("(p j) n -> p j n", j=PACK)
        w1_rows = w1.rearrange("(p j) c -> p j c", j=PACK)
        x_sb = [load("x_sb0", [P, T], F32, x_rows[:, 0, :])]
        offs_sb = load("offs_sb", [P, S // 16], U16, offs)
        x_sb.extend([load("x_sb%d" % j, [P, T], F32, x_rows[:, j, :]) for j in range(1, PACK)])
        w1_raw = [load("w1_raw%d" % a, [P, PACK, HALF_H], F32, w1_rows[:, :, a * HALF_H:(a + 1) * HALF_H]) for a in range(2)]
        w2_rows = w2.rearrange("(p j) c -> p j c", j=PACK)
        w2_raw = [load("w2_raw%d" % a, [P, PACK, HALF_H], F32, w2_rows[:, :, a * HALF_H:(a + 1) * HALF_H]) for a in range(2)]
        pos_sb = [load("pos1_sb", [P, V // 16], U16, pos1), load("pos2_sb", [P, V // 16], U16, pos2)]
        gate_rows = gate.rearrange("d p v -> p d v")
        gate_sb = [load("gate_sb%d" % v0, [P, 2, n], F32, gate_rows[:, :, v0:v0 + n]) for v0, n, own in HOP1_PARTS]
        nxt_sb = [load("nxt1_sb", [P, U // 16], U16, nxt1), load("nxt2_sb", [P, U // 16], U16, nxt2)]
        gate2_rows = gate2.rearrange("d p r -> p d r")
        gate2_sb = [load("gate2_sb%d" % r0, [P, 2, n], F32, gate2_rows[:, :, r0:r0 + n]) for r0, n, own in HOP2_PARTS]

        x_bf = [sb.tile([P, HALF_S * PACK], BF16, name="x_bf%d" % a, align_bytes=64) for a in range(2)]
        cols = HALF_S // 16
        for pair in range(2):
            picked = sb.tile([P, 2, HALF_S], BF16, name="x_picked%d" % pair)
            for e in range(2):
                j = 2 * pair + e
                nc.vector.tensor_copy(x_bf[0][:].rearrange("p (n j) -> p n j", j=PACK)[:, :, j], x_sb[j][:].indirect(offs_sb[:, 0:cols]))
                nc.scalar.activation(picked[:, e, :], x_sb[j][:].indirect(offs_sb[:, cols:2 * cols]), ACT.Copy)
            nc.vector.tensor_copy(
                x_bf[1][:].rearrange("p (n j) -> p n j", j=PACK)[:, :, 2 * pair:2 * pair + 2],
                picked[:].rearrange("p e n -> p n e"))
        x_mx = [mx_tiles("x0", HALF_S, "x_sb3"), mx_tiles("x1", HALF_S)]
        for a in range(2):
            quantise(x_mx[a][0][:], x_mx[a][1][:], x_bf[a][:])

        w1_bf = sb.tile([P, H * PACK], BF16, name="w1_bf", align_bytes=64)
        deal(nc.scalar.copy, w1_bf, w1_raw[0], 0, P // 2)
        for t in range(0, PACK, 2):
            deal(nc.scalar.copy, w1_bf, w1_raw[1], P // 2, P // 2, slice(t, t + 2))
        w1_codes, w1_scales = mx_tiles("w1", H)
        for t in range(PACK):
            quantise(w1_codes[:, t * P:(t + 1) * P], w1_scales[:, t * P:(t + 1) * P], w1_bf[:, t * H:(t + 1) * H])

        w2_bf = sb.tile([P, H * PACK], BF16, name="w2_bf", align_bytes=64)
        deal(nc.vector.tensor_copy, w2_bf, w2_raw[0], 0, P // 2)
        deal(nc.vector.tensor_copy, w2_bf, w2_raw[1], P // 2, P // 2)
        w2_codes, w2_scales = mx_tiles("w2", H)
        quantise(w2_codes[:], w2_scales[:], w2_bf[:])

        def product(bank, width, w_codes, w_scales, t, moving):
            acc = ps.tile([P, width], F32, name="acc", tag="bank%d" % bank)
            for c0, c1 in {384: [(0, 256), (256, 384)], 192: [(0, 128), (128, 192)]}.get(width, [(0, width)]):
                nc.tensor.matmul_mx(
                    out=acc[:, c0:c1], lhsT=w_codes[:, t * P:(t + 1) * P].bitcast(FP8X4), lhsT_scale=w_scales[:, t * P:(t + 1) * P],
                    rhs=moving[0][:, c0:c1].bitcast(FP8X4), rhs_scale=moving[1][:, c0:c1], start=True, stop=True)
            return acc

        h_sb = [sb.tile([P, S], F32, name="h_sb%d" % t) for t in range(PACK)]
        for t in range(PACK):
            for a in range(2):
                acc = product(2 * t + a, HALF_S, w1_codes, w1_scales, t, x_mx[a])
                relu(2 * t + a in H_BANKS_ON_VECTOR, h_sb[t][:, a * HALF_S:(a + 1) * HALF_S], acc[:])

        def weighted_terms(name, windows, lists, first, count, own, weights):
            terms = sb.tile([P, PACK, 2, count], F32, name=name + "_terms")
            plain = sb.tile([P, PACK, 2, count], F32, name=name + "_plain")
            cols = slice(first // 16, (first + count) // 16)
            jobs = [(t, d) for t in range(PACK) for d in range(2)]
            for t, d in jobs:
                if (t, d) in own:
                    nc.vector.tensor_tensor(terms[:, t, d, :], windows[t][:].indirect(lists[d][:, cols]), weights[:, d, :], ALU.mult)
                else:
                    nc.scalar.activation(plain[:, t, d, :], windows[t][:].indirect(lists[d][:, cols]), ACT.Copy)
            for t in range(PACK):
                rest = [d for d in range(2) if (t, d) not in own]
                if rest:
                    ds = slice(rest[0], rest[-1] + 1)
                    nc.vector.tensor_tensor(terms[:, t, ds, :], plain[:, t, ds, :], weights[:, ds, :], ALU.mult)
            return terms[:, :, 0, :], terms[:, :, 1, :]

        g_sb = [sb.tile([P, V], F32, name="g_sb%d" % t) for t in range(PACK)]
        g_acc = []
        for a, (v0, n, own) in enumerate(HOP1_PARTS):
            terms = weighted_terms("z%d" % a, h_sb, pos_sb, v0, n, own, gate_sb[a])
            z_bf = sb.tile([P, n * PACK], BF16, name="z_bf%d" % a, align_bytes=64)
            nc.vector.tensor_tensor(
                z_bf[:].rearrange("p (c i t) -> p c t i", i=2, t=PACK),
                terms[0].rearrange("p t (c i) -> p c t i", i=2),
                terms[1].rearrange("p t (c i) -> p c t i", i=2), ALU.add)
            z_mx = mx_tiles("z%d" % a, n)
            quantise(z_mx[0][:], z_mx[1][:], z_bf[:])
            g_acc.append([product((PACK * a + t) % 8, n, w2_codes, w2_scales, t, z_mx) for t in range(PACK)])
            pass
        for a, (v0, n, own) in enumerate(HOP1_PARTS):
            last = a == len(HOP1_PARTS) - 1
            if last or True:
                for t in range(PACK):
                    relu(last and t in G_BANKS_ON_VECTOR, g_sb[t][:, v0:v0 + n], g_acc[a][t][:])

        y_rows = out_0.rearrange("(p t) r -> p t r", t=PACK)
        y_codes, y_scales = mx_tiles("y", U)
        word_rows = out_1[0].rearrange("l c r -> l (c r)").bitcast(I32)
        for a, (r0, n, own) in enumerate(HOP2_PARTS):
            terms = weighted_terms("y%d" % a, g_sb, nxt_sb, r0, n, own, gate2_sb[a])
            y_sb = sb.tile([P, PACK, n], F32, name="y_sb%d" % a)
            nc.vector.tensor_tensor(y_sb[:], terms[0], terms[1], ALU.add)
            nc.sync.dma_start(y_rows[:, :, r0:r0 + n], y_sb[:])
            y_bf = sb.tile([P, n * PACK], BF16, name="y_bf%d" % a, align_bytes=64)
            copy = nc.vector.tensor_copy if a == len(HOP2_PARTS) - 1 else nc.scalar.copy
            copy(y_bf[:].rearrange("p (c i t) -> p c t i", i=2, t=PACK), y_sb[:].rearrange("p t (c i) -> p c t i", i=2))
            quantise(y_codes[:, r0:r0 + n], y_scales[:, r0:r0 + n], y_bf[:])
        nc.sync.dma_start(word_rows, y_codes[:].bitcast(I32))
        scale_rows = out_2[0].bitcast(I32)
        for q in range(4):
            queue = nc.sync if q % 2 else nc.scalar
            queue.dma_start(scale_rows[4 * q:4 * q + 4, :], y_scales[:].bitcast(I32)[32 * q:32 * q + 4, :])
